import numpy as np
import ml_dtypes

BF16 = ml_dtypes.bfloat16


def bf(x):
    return np.asarray(x, np.float32).astype(BF16)


def f32(x):
    return np.asarray(x, np.float32)


def f64(x):
    return np.asarray(x).astype(np.float64)


def striped(idx):
    return np.tile(idx.reshape(-1, 16).T, (8, 1))


def rows(idx, k):
    return np.tile(idx, (k, 1))


def look(tab, idx):
    return np.take_along_axis(f64(tab), rows(idx, len(tab)), axis=1)


K, S, V, N = 128, 2048, 1536, 1536


def setup_inputs():
    return {"tab": f32(np.random.standard_normal((2, K, S))), "y": f32(np.random.standard_normal((K, V))), "offs": striped(np.random.permutation(S)[:N])}


def reference(tab, y, offs):
    idx = offs[:16].T.reshape(-1)
    x = (look(tab[0], idx) * f64(y)) * (1.0 / (1.0 + np.exp(-look(tab[1], idx))))
    return x

@@ -1,0 +1,36 @@
+import concourse.mybir as mybir
+
+F32 = mybir.dt.float32
+U16 = mybir.dt.uint16
+MULT = mybir.AluOpType.mult
+SIGMOID = mybir.ActivationFunctionType.Sigmoid
+
+ROWS = 128
+PLACES = 2048
+ENTRIES = 1536
+LANES = 16
+PIECE = 512
+
+
+def tile_lookup_vg_mulsig_out_kernel(tc, tab, y, offs, out):
+    nc = tc.nc
+    with tc.tile_pool(name="held", bufs=1) as held, tc.tile_pool(name="work", bufs=ENTRIES // PIECE) as work:
+        places = held.tile([ROWS, ENTRIES // LANES], U16, name="places")
+        values = held.tile([ROWS, PLACES], F32, name="values")
+        gates = held.tile([ROWS, PLACES], F32, name="gates")
+        stream = held.tile([ROWS, ENTRIES], F32, name="stream")
+        nc.sync.dma_start(places[:], offs)
+        nc.sync.dma_start(values[:], tab[0, :, :])
+        nc.sync.dma_start(stream[:], y)
+        nc.sync.dma_start(gates[:], tab[1, :, :])
+
+        for start in range(0, ENTRIES, PIECE):
+            stop = start + PIECE
+            piece_places = places[:, start // LANES : stop // LANES]
+            scaled = work.tile([ROWS, PIECE], F32, name="scaled")
+            gate = work.tile([ROWS, PIECE], F32, name="gate")
+            gated = work.tile([ROWS, PIECE], F32, name="gated")
+            nc.vector.tensor_tensor(scaled[:], values[:].indirect(piece_places), stream[:, start:stop], MULT)
+            nc.scalar.activation(gate[:], gates[:].indirect(piece_places), SIGMOID)
+            nc.vector.tensor_tensor(gated[:], scaled[:], gate[:], MULT)
+            nc.sync.dma_start(out[:, start:stop], gated[:])

@@ -24,6 +24,11 @@ def tile_lookup_vg_mulsig_out_kernel(tc, tab, y, offs, out):
         nc.sync.dma_start(stream[:], y)
         nc.sync.dma_start(gates[:], tab[1, :, :])
 
+        warm_in = held.tile([ROWS, 1], F32, name="warm_in")
+        warm_out = held.tile([ROWS, 1], F32, name="warm_out")
+        nc.vector.memset(warm_in[:], 0.0)
+        nc.scalar.activation(warm_out[:], warm_in[:], SIGMOID)
+
         for start in range(0, ENTRIES, PIECE):
             stop = start + PIECE
             piece_places = places[:, start // LANES : stop // LANES]

@@ -9,33 +9,38 @@ ROWS = 128
 PLACES = 2048
 ENTRIES = 1536
 LANES = 16
-PIECE = 512
+PIECE = 256
+HEAD = 1024
 
 
 def tile_lookup_vg_mulsig_out_kernel(tc, tab, y, offs, out):
     nc = tc.nc
-    with tc.tile_pool(name="held", bufs=1) as held, tc.tile_pool(name="work", bufs=ENTRIES // PIECE) as work:
+    with tc.tile_pool(name="held", bufs=1) as held:
         places = held.tile([ROWS, ENTRIES // LANES], U16, name="places")
         values = held.tile([ROWS, PLACES], F32, name="values")
         gates = held.tile([ROWS, PLACES], F32, name="gates")
         stream = held.tile([ROWS, ENTRIES], F32, name="stream")
+        scaled = held.tile([ROWS, ENTRIES], F32, name="scaled")
+        gate = held.tile([ROWS, ENTRIES], F32, name="gate")
+        gated = held.tile([ROWS, ENTRIES], F32, name="gated")
+
         nc.sync.dma_start(places[:], offs)
         nc.sync.dma_start(values[:], tab[0, :, :])
-        nc.sync.dma_start(stream[:], y)
+        nc.sync.dma_start(stream[:, :HEAD], y[:, :HEAD])
         nc.sync.dma_start(gates[:], tab[1, :, :])
+        nc.sync.dma_start(stream[:, HEAD:], y[:, HEAD:])
 
         warm_in = held.tile([ROWS, 1], F32, name="warm_in")
         warm_out = held.tile([ROWS, 1], F32, name="warm_out")
         nc.vector.memset(warm_in[:], 0.0)
         nc.scalar.activation(warm_out[:], warm_in[:], SIGMOID)
 
-        for start in range(0, ENTRIES, PIECE):
-            stop = start + PIECE
-            piece_places = places[:, start // LANES : stop // LANES]
-            scaled = work.tile([ROWS, PIECE], F32, name="scaled")
-            gate = work.tile([ROWS, PIECE], F32, name="gate")
-            gated = work.tile([ROWS, PIECE], F32, name="gated")
-            nc.vector.tensor_tensor(scaled[:], values[:].indirect(piece_places), stream[:, start:stop], MULT)
-            nc.scalar.activation(gate[:], gates[:].indirect(piece_places), SIGMOID)
-            nc.vector.tensor_tensor(gated[:], scaled[:], gate[:], MULT)
-            nc.sync.dma_start(out[:, start:stop], gated[:])
+        pieces = [slice(start, start + PIECE) for start in range(0, ENTRIES, PIECE)]
+        for piece in pieces:
+            listed = places[:, piece.start // LANES : piece.stop // LANES]
+            nc.vector.tensor_tensor(scaled[:, piece], values[:].indirect(listed), stream[:, piece], MULT)
+        for piece in pieces:
+            listed = places[:, piece.start // LANES : piece.stop // LANES]
+            nc.scalar.activation(gate[:, piece], gates[:].indirect(listed), SIGMOID)
+            nc.vector.tensor_tensor(gated[:, piece], scaled[:, piece], gate[:, piece], MULT)
+            nc.sync.dma_start(out[:, piece], gated[:, piece])

@@ -9,8 +9,9 @@ ROWS = 128
 PLACES = 2048
 ENTRIES = 1536
 LANES = 16
-PIECE = 256
-HEAD = 1024
+PIECE = 384
+LOAD = 384
+HEAD = 768
 
 
 def tile_lookup_vg_mulsig_out_kernel(tc, tab, y, offs, out):
@@ -26,9 +27,11 @@ def tile_lookup_vg_mulsig_out_kernel(tc, tab, y, offs, out):
 
         nc.sync.dma_start(places[:], offs)
         nc.sync.dma_start(values[:], tab[0, :, :])
-        nc.sync.dma_start(stream[:, :HEAD], y[:, :HEAD])
+        for start in range(0, HEAD, LOAD):
+            nc.sync.dma_start(stream[:, start : start + LOAD], y[:, start : start + LOAD])
         nc.sync.dma_start(gates[:], tab[1, :, :])
-        nc.sync.dma_start(stream[:, HEAD:], y[:, HEAD:])
+        for start in range(HEAD, ENTRIES, LOAD):
+            nc.sync.dma_start(stream[:, start : start + LOAD], y[:, start : start + LOAD])
 
         warm_in = held.tile([ROWS, 1], F32, name="warm_in")
         warm_out = held.tile([ROWS, 1], F32, name="warm_out")

import concourse.mybir as mybir

F32 = mybir.dt.float32
U16 = mybir.dt.uint16
MULT = mybir.AluOpType.mult
SIGMOID = mybir.ActivationFunctionType.Sigmoid

ROWS = 128
PLACES = 2048
ENTRIES = 1536
LANES = 16
PIECE = 384
LOAD = 384
HEAD = 768


def tile_lookup_vg_mulsig_out_kernel(tc, tab, y, offs, out):
    nc = tc.nc
    with tc.tile_pool(name="held", bufs=1) as held:
        places = held.tile([ROWS, ENTRIES // LANES], U16, name="places")
        values = held.tile([ROWS, PLACES], F32, name="values")
        gates = held.tile([ROWS, PLACES], F32, name="gates")
        stream = held.tile([ROWS, ENTRIES], F32, name="stream")
        scaled = held.tile([ROWS, ENTRIES], F32, name="scaled")
        gate = held.tile([ROWS, ENTRIES], F32, name="gate")
        gated = held.tile([ROWS, ENTRIES], F32, name="gated")

        nc.sync.dma_start(places[:], offs)
        nc.sync.dma_start(values[:], tab[0, :, :])
        for start in range(0, HEAD, LOAD):
            nc.sync.dma_start(stream[:, start : start + LOAD], y[:, start : start + LOAD])
        nc.sync.dma_start(gates[:], tab[1, :, :])
        for start in range(HEAD, ENTRIES, LOAD):
            nc.sync.dma_start(stream[:, start : start + LOAD], y[:, start : start + LOAD])

        warm_in = held.tile([ROWS, 1], F32, name="warm_in")
        warm_out = held.tile([ROWS, 1], F32, name="warm_out")
        nc.vector.memset(warm_in[:], 0.0)
        nc.scalar.activation(warm_out[:], warm_in[:], SIGMOID)

        pieces = [slice(start, start + PIECE) for start in range(0, ENTRIES, PIECE)]
        for piece in pieces:
            listed = places[:, piece.start // LANES : piece.stop // LANES]
            nc.vector.tensor_tensor(scaled[:, piece], values[:].indirect(listed), stream[:, piece], MULT)
        for piece in pieces:
            listed = places[:, piece.start // LANES : piece.stop // LANES]
            nc.scalar.activation(gate[:, piece], gates[:].indirect(listed), SIGMOID)
            nc.vector.tensor_tensor(gated[:, piece], scaled[:, piece], gate[:, piece], MULT)
            nc.sync.dma_start(out[:, piece], gated[:, piece])
